import numpy as np
import ml_dtypes


def mxq(x, axis, fmt="e4m3"):
    dtype, down = {"e4m3": (ml_dtypes.float8_e4m3fn, 7), "e5m2": (ml_dtypes.float8_e5m2, 14)}[fmt]
    v = np.moveaxis(np.asarray(x, np.float32).astype(ml_dtypes.bfloat16).astype(np.float64), axis, -1)
    blocks = v.reshape(v.shape[:-1] + (-1, 32))
    amax = np.abs(blocks).max(-1, keepdims=True)
    byte = np.maximum(np.where(amax > 0, np.frexp(amax)[1] - 1 + 127, 0) - down, 1)
    scale = np.exp2(byte - 127.0)
    codes = (blocks / scale).astype(np.float32).astype(dtype).astype(np.float64)
    return np.moveaxis((codes * scale).reshape(v.shape), -1, axis)


WIDE = False


def mx_kscale(k):
    if not WIDE:
        return np.ones(k)
    levels = np.array([10, -10, 5, -5, 0])
    if k % 512:
        return np.exp2(np.random.permutation(np.resize(levels, k // 32))).repeat(32)
    a = np.empty((k // 512, 16))
    for p in range(k // 512):
        a[p, :8] = np.random.permutation(np.resize(levels, 8))
        for g in range(8):
            far = levels[np.abs(levels - a[p, g]) >= 10]
            a[p, g + 8] = far[np.random.randint(len(far))]
    return np.exp2(a.ravel()).repeat(32)


def f64(x):
    return np.asarray(x).astype(np.float64)


def striped(idx):
    return np.tile(idx.reshape(-1, 16).T, (8, 1)).astype(np.uint16)


def unstriped(offs):
    return offs[:16].T.reshape(-1).astype(np.int64)


def pack_weight(w):
    k, n = w.shape
    w = f64(np.asarray(w, np.float32).astype(ml_dtypes.bfloat16)).reshape(k // 32, 32, n)
    amax = np.abs(w).max(1)
    byte = np.clip(np.where(amax > 0, np.frexp(amax)[1] - 1 + 127 - 7, 1), 1, 254)
    scaled = (w * np.exp2(127.0 - byte)[:, None, :]).reshape(k, n).astype(np.float32)
    words = np.ascontiguousarray(scaled.reshape(k // 512, 128, 4, n).transpose(0, 1, 3, 2)).astype(ml_dtypes.float8_e4m3fn).view(np.uint8)
    return words, np.ascontiguousarray(byte.astype(np.uint8).reshape(k // 512, 16, n))


def unpack_weight(words, scales):
    g, p, n, _ = words.shape
    vals = np.ascontiguousarray(words).view(ml_dtypes.float8_e4m3fn).astype(np.float64) * np.repeat(np.exp2(scales.astype(np.float64) - 127.0), 8, axis=1)[..., None]
    return vals.transpose(0, 1, 3, 2).reshape(g * 512, n)


def sigmoid(v):
    return 1.0 / (1.0 + np.exp(-np.maximum(v, -700.0)))


K, T, S, J = 512, 1024, 512, 512


def setup_inputs():
    n = np.random.standard_normal
    s = mx_kscale(K)[:, None]
    packed_xT = pack_weight(n((K, T)) * s)
    return {
        "x_words": packed_xT[0],
        "x_scales": packed_xT[1],
        "hT": (n((K, J)) / np.sqrt(K) / s).astype(np.float32),
        "label": (np.random.uniform(0.0, 0.4, (J, S))).astype(np.float32),
        "offs": striped(np.random.permutation(T)[:S]),
    }


def reference(x_words, x_scales, hT, label, offs):
    hTq = mxq(f64(hT), 0, "e4m3")
    xq = unpack_weight(x_words, x_scales)[:, unstriped(offs)]
    z = 4.0 * ((hTq.T @ xq) - f64(label))
    return sigmoid(z)

@@ -1,0 +1,110 @@
+from contextlib import ExitStack
+
+import concourse.mybir as mybir
+
+K, T, S, J = 512, 1024, 512, 512
+FLOPS = 2 * K * S * J
+
+F32 = mybir.dt.float32
+BF16 = mybir.dt.bfloat16
+I32 = mybir.dt.int32
+U32 = mybir.dt.uint32
+U16 = mybir.dt.uint16
+U8 = mybir.dt.uint8
+FP8X4 = mybir.dt.float8_e4m3fn_x4
+ACT = mybir.ActivationFunctionType
+ALU = mybir.AluOpType
+
+P = 128
+PACK = 4
+M_TILES = J // P
+HALF = S // 2
+H_LOADS = 2
+H_WIDTH = J // H_LOADS
+
+
+def tile_picked_zams_sig_p_kernel(tc, x_words, x_scales, hT, label, offs, out):
+    nc = tc.nc
+    with ExitStack() as ctx:
+        keep = ctx.enter_context(tc.tile_pool(name="keep", bufs=1))
+        psum = ctx.enter_context(tc.psum_pool(name="psum", bufs=1))
+
+        offsets = keep.tile([P, S // 16], U16, name="offsets")
+        table_words = keep.tile([P, T], U32, name="table_words", align_bytes=64)
+        table_bytes = keep.tile([P, T], U8, name="table_bytes", align_bytes=64)
+        picked_words = keep.tile([P, S], U32, name="picked_words", align_bytes=64)
+        picked_bytes = keep.tile([P, S], U8, name="picked_bytes", align_bytes=64)
+        warm_in = keep.tile([P, 1], F32, name="warm_in")
+        warm_out = keep.tile([P, 1], F32, name="warm_out")
+
+        nc.vector.memset(table_bytes[:].bitcast(I32), 0)
+        nc.vector.memset(warm_in[:], 0.0)
+        nc.scalar.activation(warm_out[:], warm_in[:], ACT.Sigmoid, scale=4.0)
+
+        nc.sync.dma_start(offsets[:], offs)
+        nc.sync.dma_start(table_words[:].bitcast(I32), x_words[0].rearrange("p n t -> p (n t)").bitcast(I32))
+        for q in range(4):
+            nc.sync.dma_start(table_bytes[32 * q : 32 * q + 4, :].bitcast(I32), x_scales[0, 4 * q : 4 * q + 4, :].bitcast(I32))
+
+        h_rows = hT.rearrange("(p t) c -> p t c", t=PACK)
+        h_raw = []
+        for u in range(H_LOADS):
+            raw = keep.tile([P, PACK, H_WIDTH], F32, name=f"h_raw{u}")
+            nc.sync.dma_start(raw[:], h_rows[:, :, u * H_WIDTH : (u + 1) * H_WIDTH])
+            h_raw.append(raw)
+        margins = []
+        for m in range(M_TILES):
+            margin = keep.tile([P, S], F32, name=f"margin{m}")
+            nc.sync.dma_start(margin[:], label[m * P : (m + 1) * P, :])
+            margins.append(margin)
+
+        grouped, codes, scales = [], [], []
+        for m in range(M_TILES):
+            g = keep.tile([P, P, PACK], BF16, name=f"grouped{m}", align_bytes=64)
+            u, c0 = divmod(m * P, H_WIDTH)
+            nc.scalar.copy(
+                g[:].rearrange("p (c i) t -> p c t i", i=4),
+                h_raw[u][:, :, c0 : c0 + P].rearrange("p t (c i) -> p c t i", i=4),
+            )
+            grouped.append(g)
+            codes.append(keep.tile([P, P], U32, name=f"codes{m}", align_bytes=64))
+            scales.append(keep.tile([P, P], U8, name=f"scales{m}", align_bytes=64))
+
+        def quantize(m):
+            nc.vector.quantize_mx(
+                out=codes[m][:].bitcast(FP8X4), scales=scales[m][:], in_=grouped[m][:].rearrange("p c t -> p (c t)")
+            )
+
+        def gather_bytes(lo, hi):
+            nc.vector.tensor_copy(picked_bytes[:, lo:hi], table_bytes[:].indirect(offsets[:, lo // 16 : hi // 16]))
+
+        def score(m, lo, hi):
+            acc = psum.tile([P, hi - lo], F32, name=f"acc{m}_{lo}")
+            nc.tensor.matmul_mx(
+                out=acc[:],
+                lhsT=codes[m][:].bitcast(FP8X4),
+                lhsT_scale=scales[m][:],
+                rhs=picked_words[:, lo:hi].bitcast(FP8X4),
+                rhs_scale=picked_bytes[:, lo:hi],
+                start=True,
+                stop=True,
+            )
+            z = keep.tile([P, hi - lo], F32, name=f"z{m}_{lo}")
+            nc.vector.tensor_tensor(z[:], acc[:], margins[m][:, lo:hi], ALU.subtract)
+            y = keep.tile([P, hi - lo], F32, name=f"y{m}_{lo}")
+            nc.scalar.activation(y[:], z[:], ACT.Sigmoid, scale=4.0)
+            nc.sync.dma_start(out[m * P : (m + 1) * P, lo:hi], y[:])
+
+        nc.vector.tensor_copy(picked_words[:], table_words[:].indirect(offsets[:]))
+        gather_bytes(0, HALF)
+        quantize(0)
+        gather_bytes(HALF, S)
+        quantize(1)
+        score(0, 0, HALF)
+        score(0, HALF, S)
+        quantize(2)
+        score(1, 0, S)
+        quantize(3)
+        score(2, 0, S)
+        score(3, 0, HALF)
+        score(3, HALF, S)

@@ -33,78 +33,99 @@ def tile_picked_zams_sig_p_kernel(tc, x_words, x_scales, hT, label, offs, out):
         table_words = keep.tile([P, T], U32, name="table_words", align_bytes=64)
         table_bytes = keep.tile([P, T], U8, name="table_bytes", align_bytes=64)
         picked_words = keep.tile([P, S], U32, name="picked_words", align_bytes=64)
-        picked_bytes = keep.tile([P, S], U8, name="picked_bytes", align_bytes=64)
         warm_in = keep.tile([P, 1], F32, name="warm_in")
         warm_out = keep.tile([P, 1], F32, name="warm_out")
 
         nc.vector.memset(table_bytes[:].bitcast(I32), 0)
         nc.vector.memset(warm_in[:], 0.0)
-        nc.scalar.activation(warm_out[:], warm_in[:], ACT.Sigmoid, scale=4.0)
-
-        nc.sync.dma_start(offsets[:], offs)
+        h_rows = hT.rearrange("(p t) c -> p t c", t=PACK)
         nc.sync.dma_start(table_words[:].bitcast(I32), x_words[0].rearrange("p n t -> p (n t)").bitcast(I32))
+        nc.sync.dma_start(offsets[:], offs)
         for q in range(4):
             nc.sync.dma_start(table_bytes[32 * q : 32 * q + 4, :].bitcast(I32), x_scales[0, 4 * q : 4 * q + 4, :].bitcast(I32))
-
-        h_rows = hT.rearrange("(p t) c -> p t c", t=PACK)
-        h_raw = []
-        for u in range(H_LOADS):
-            raw = keep.tile([P, PACK, H_WIDTH], F32, name=f"h_raw{u}")
-            nc.sync.dma_start(raw[:], h_rows[:, :, u * H_WIDTH : (u + 1) * H_WIDTH])
-            h_raw.append(raw)
-        margins = []
-        for m in range(M_TILES):
-            margin = keep.tile([P, S], F32, name=f"margin{m}")
-            nc.sync.dma_start(margin[:], label[m * P : (m + 1) * P, :])
-            margins.append(margin)
-
-        grouped, codes, scales = [], [], []
-        for m in range(M_TILES):
-            g = keep.tile([P, P, PACK], BF16, name=f"grouped{m}", align_bytes=64)
-            u, c0 = divmod(m * P, H_WIDTH)
-            nc.scalar.copy(
-                g[:].rearrange("p (c i) t -> p c t i", i=4),
-                h_raw[u][:, :, c0 : c0 + P].rearrange("p t (c i) -> p c t i", i=4),
-            )
-            grouped.append(g)
-            codes.append(keep.tile([P, P], U32, name=f"codes{m}", align_bytes=64))
-            scales.append(keep.tile([P, P], U8, name=f"scales{m}", align_bytes=64))
-
-        def quantize(m):
-            nc.vector.quantize_mx(
-                out=codes[m][:].bitcast(FP8X4), scales=scales[m][:], in_=grouped[m][:].rearrange("p c t -> p (c t)")
-            )
-
-        def gather_bytes(lo, hi):
-            nc.vector.tensor_copy(picked_bytes[:, lo:hi], table_bytes[:].indirect(offsets[:, lo // 16 : hi // 16]))
-
-        def score(m, lo, hi):
-            acc = psum.tile([P, hi - lo], F32, name=f"acc{m}_{lo}")
-            nc.tensor.matmul_mx(
-                out=acc[:],
-                lhsT=codes[m][:].bitcast(FP8X4),
-                lhsT_scale=scales[m][:],
-                rhs=picked_words[:, lo:hi].bitcast(FP8X4),
-                rhs_scale=picked_bytes[:, lo:hi],
-                start=True,
-                stop=True,
-            )
-            z = keep.tile([P, hi - lo], F32, name=f"z{m}_{lo}")
-            nc.vector.tensor_tensor(z[:], acc[:], margins[m][:, lo:hi], ALU.subtract)
-            y = keep.tile([P, hi - lo], F32, name=f"y{m}_{lo}")
-            nc.scalar.activation(y[:], z[:], ACT.Sigmoid, scale=4.0)
-            nc.sync.dma_start(out[m * P : (m + 1) * P, lo:hi], y[:])
-
+        h0 = keep.tile([P, PACK, 128], F32, name="h0", tag="h0", align_bytes=64)
+        nc.sync.dma_start(h0[:], h_rows[:, :, 0:128])
+        h1 = keep.tile([P, PACK, 256], F32, name="h1", tag="h1", align_bytes=64)
+        nc.sync.dma_start(h1[:], h_rows[:, :, 128:384])
+        h2 = keep.tile([P, PACK, 128], F32, name="h2", tag="h2", align_bytes=64)
+        nc.sync.dma_start(h2[:], h_rows[:, :, 384:512])
+        l0_0 = keep.tile([P, 512], F32, name="l0_0")
+        nc.sync.dma_start(l0_0[:], label[0:128, 0:512])
+        l1_0 = keep.tile([P, 512], F32, name="l1_0")
+        nc.sync.dma_start(l1_0[:], label[128:256, 0:512])
+        l2_0 = keep.tile([P, 512], F32, name="l2_0")
+        nc.sync.dma_start(l2_0[:], label[256:384, 0:512])
+        l3_0 = keep.tile([P, 256], F32, name="l3_0")
+        nc.sync.dma_start(l3_0[:], label[384:512, 0:256])
+        l3_256 = keep.tile([P, 256], F32, name="l3_256")
+        nc.sync.dma_start(l3_256[:], label[384:512, 256:512])
+        nc.scalar.activation(warm_out[:], warm_in[:], ACT.Sigmoid, scale=4.0)
+        grouped = [keep.tile([P, P, PACK], BF16, name=f"grouped{m}", tag=f"grouped{m}", align_bytes=64) for m in range(4)]
+        codes = [keep.tile([P, P], U32, name=f"codes{m}", align_bytes=64) for m in range(4)]
+        scales = [keep.tile([P, P], U8, name=f"scales{m}", align_bytes=64) for m in range(4)]
+        nc.scalar.copy(grouped[0][:].rearrange("p (c i) t -> p c t i", i=4), h0[:, :, 0:128].rearrange("p t (c i) -> p c t i", i=4))
         nc.vector.tensor_copy(picked_words[:], table_words[:].indirect(offsets[:]))
-        gather_bytes(0, HALF)
-        quantize(0)
-        gather_bytes(HALF, S)
-        quantize(1)
-        score(0, 0, HALF)
-        score(0, HALF, S)
-        quantize(2)
-        score(1, 0, S)
-        quantize(3)
-        score(2, 0, S)
-        score(3, 0, HALF)
-        score(3, HALF, S)
+        picked_bytes0 = keep.tile([P, 256], U8, name="picked_bytes0", tag="picked_bytes0", align_bytes=64)
+        nc.vector.tensor_copy(picked_bytes0[:], table_bytes[:].indirect(offsets[:, 0:16]))
+        nc.vector.quantize_mx(out=codes[0][:].bitcast(FP8X4), scales=scales[0][:], in_=grouped[0][:].rearrange("p c t -> p (c t)"))
+        picked_bytes1 = keep.tile([P, 256], U8, name="picked_bytes1", tag="h0", align_bytes=64)
+        nc.vector.tensor_copy(picked_bytes1[:], table_bytes[:].indirect(offsets[:, 16:32]))
+        acc0_0 = psum.tile([P, 256], F32, name="acc0_0")
+        nc.tensor.matmul_mx(out=acc0_0[:, 0:256], lhsT=codes[0][:].bitcast(FP8X4), lhsT_scale=scales[0][:], rhs=picked_words[:, 0:256].bitcast(FP8X4), rhs_scale=picked_bytes0[:], start=True, stop=True)
+        acc0_1 = psum.tile([P, 256], F32, name="acc0_1")
+        nc.tensor.matmul_mx(out=acc0_1[:, 0:256], lhsT=codes[0][:].bitcast(FP8X4), lhsT_scale=scales[0][:], rhs=picked_words[:, 256:512].bitcast(FP8X4), rhs_scale=picked_bytes1[:], start=True, stop=True)
+        nc.scalar.copy(grouped[1][:].rearrange("p (c i) t -> p c t i", i=4), h1[:, :, 0:128].rearrange("p t (c i) -> p c t i", i=4))
+        nc.vector.quantize_mx(out=codes[1][:].bitcast(FP8X4), scales=scales[1][:], in_=grouped[1][:].rearrange("p c t -> p (c t)"))
+        acc1 = psum.tile([P, 512], F32, name="acc1")
+        nc.tensor.matmul_mx(out=acc1[:, 0:256], lhsT=codes[1][:].bitcast(FP8X4), lhsT_scale=scales[1][:], rhs=picked_words[:, 0:256].bitcast(FP8X4), rhs_scale=picked_bytes0[:], start=True, stop=True)
+        nc.tensor.matmul_mx(out=acc1[:, 256:512], lhsT=codes[1][:].bitcast(FP8X4), lhsT_scale=scales[1][:], rhs=picked_words[:, 256:512].bitcast(FP8X4), rhs_scale=picked_bytes1[:], start=True, stop=True)
+        nc.scalar.copy(grouped[2][:].rearrange("p (c i) t -> p c t i", i=4), h1[:, :, 128:256].rearrange("p t (c i) -> p c t i", i=4))
+        nc.vector.quantize_mx(out=codes[2][:].bitcast(FP8X4), scales=scales[2][:], in_=grouped[2][:].rearrange("p c t -> p (c t)"))
+        acc2 = psum.tile([P, 512], F32, name="acc2")
+        nc.tensor.matmul_mx(out=acc2[:, 0:256], lhsT=codes[2][:].bitcast(FP8X4), lhsT_scale=scales[2][:], rhs=picked_words[:, 0:256].bitcast(FP8X4), rhs_scale=picked_bytes0[:], start=True, stop=True)
+        nc.tensor.matmul_mx(out=acc2[:, 256:512], lhsT=codes[2][:].bitcast(FP8X4), lhsT_scale=scales[2][:], rhs=picked_words[:, 256:512].bitcast(FP8X4), rhs_scale=picked_bytes1[:], start=True, stop=True)
+        nc.scalar.copy(grouped[3][:].rearrange("p (c i) t -> p c t i", i=4), h2[:, :, 0:128].rearrange("p t (c i) -> p c t i", i=4))
+        nc.vector.quantize_mx(out=codes[3][:].bitcast(FP8X4), scales=scales[3][:], in_=grouped[3][:].rearrange("p c t -> p (c t)"))
+        acc3 = psum.tile([P, 512], F32, name="acc3")
+        nc.tensor.matmul_mx(out=acc3[:, 0:256], lhsT=codes[3][:].bitcast(FP8X4), lhsT_scale=scales[3][:], rhs=picked_words[:, 0:256].bitcast(FP8X4), rhs_scale=picked_bytes0[:], start=True, stop=True)
+        nc.tensor.matmul_mx(out=acc3[:, 256:512], lhsT=codes[3][:].bitcast(FP8X4), lhsT_scale=scales[3][:], rhs=picked_words[:, 256:512].bitcast(FP8X4), rhs_scale=picked_bytes1[:], start=True, stop=True)
+        z0_0 = keep.tile([P, 256], F32, name="z0_0")
+        y0_0 = keep.tile([P, 256], F32, name="y0_0")
+        nc.vector.tensor_tensor(z0_0[:], acc0_0[:, 0:256], l0_0[:, 0:256], ALU.subtract)
+        nc.scalar.activation(y0_0[:], z0_0[:], ACT.Sigmoid, scale=4.0)
+        nc.sync.dma_start(out[0:128, 0:256], y0_0[:])
+        z0_256 = keep.tile([P, 256], F32, name="z0_256")
+        y0_256 = keep.tile([P, 256], F32, name="y0_256")
+        nc.vector.tensor_tensor(z0_256[:], acc0_1[:, 0:256], l0_0[:, 256:512], ALU.subtract)
+        nc.scalar.activation(y0_256[:], z0_256[:], ACT.Sigmoid, scale=4.0)
+        nc.sync.dma_start(out[0:128, 256:512], y0_256[:])
+        z1_0 = keep.tile([P, 256], F32, name="z1_0")
+        y1_0 = keep.tile([P, 256], F32, name="y1_0")
+        nc.vector.tensor_tensor(z1_0[:], acc1[:, 0:256], l1_0[:, 0:256], ALU.subtract)
+        nc.scalar.activation(y1_0[:], z1_0[:], ACT.Sigmoid, scale=4.0)
+        nc.sync.dma_start(out[128:256, 0:256], y1_0[:])
+        z1_256 = keep.tile([P, 256], F32, name="z1_256")
+        y1_256 = keep.tile([P, 256], F32, name="y1_256")
+        nc.vector.tensor_tensor(z1_256[:], acc1[:, 256:512], l1_0[:, 256:512], ALU.subtract)
+        nc.scalar.activation(y1_256[:], z1_256[:], ACT.Sigmoid, scale=4.0)
+        nc.sync.dma_start(out[128:256, 256:512], y1_256[:])
+        z2_0 = keep.tile([P, 256], F32, name="z2_0")
+        y2_0 = keep.tile([P, 256], F32, name="y2_0")
+        nc.vector.tensor_tensor(z2_0[:], acc2[:, 0:256], l2_0[:, 0:256], ALU.subtract)
+        nc.scalar.activation(y2_0[:], z2_0[:], ACT.Sigmoid, scale=4.0)
+        nc.sync.dma_start(out[256:384, 0:256], y2_0[:])
+        z2_256 = keep.tile([P, 256], F32, name="z2_256")
+        y2_256 = keep.tile([P, 256], F32, name="y2_256")
+        nc.vector.tensor_tensor(z2_256[:], acc2[:, 256:512], l2_0[:, 256:512], ALU.subtract)
+        nc.scalar.activation(y2_256[:], z2_256[:], ACT.Sigmoid, scale=4.0)
+        nc.sync.dma_start(out[256:384, 256:512], y2_256[:])
+        z3_0 = keep.tile([P, 256], F32, name="z3_0")
+        y3_0 = keep.tile([P, 256], F32, name="y3_0")
+        nc.vector.tensor_tensor(z3_0[:], acc3[:, 0:256], l3_0[:, 0:256], ALU.subtract)
+        nc.scalar.activation(y3_0[:], z3_0[:], ACT.Sigmoid, scale=4.0)
+        nc.sync.dma_start(out[384:512, 0:256], y3_0[:])
+        z3_256 = keep.tile([P, 256], F32, name="z3_256")
+        y3_256 = keep.tile([P, 256], F32, name="y3_256")
+        nc.vector.tensor_tensor(z3_256[:], acc3[:, 256:512], l3_256[:, 0:256], ALU.subtract)
+        nc.scalar.activation(y3_256[:], z3_256[:], ACT.Sigmoid, scale=4.0)
+        nc.sync.dma_start(out[384:512, 256:512], y3_256[:])

@@ -75,20 +75,23 @@ def tile_picked_zams_sig_p_kernel(tc, x_words, x_scales, hT, label, offs, out):
         acc0_1 = psum.tile([P, 256], F32, name="acc0_1")
         nc.tensor.matmul_mx(out=acc0_1[:, 0:256], lhsT=codes[0][:].bitcast(FP8X4), lhsT_scale=scales[0][:], rhs=picked_words[:, 256:512].bitcast(FP8X4), rhs_scale=picked_bytes1[:], start=True, stop=True)
         nc.scalar.copy(grouped[1][:].rearrange("p (c i) t -> p c t i", i=4), h1[:, :, 0:128].rearrange("p t (c i) -> p c t i", i=4))
+        nc.gpsimd.tensor_scalar(grouped[2][:], h1[:, :, 128:256].rearrange("p t c -> p c t"), 1.0, 0.0, ALU.mult, ALU.add)
         nc.vector.quantize_mx(out=codes[1][:].bitcast(FP8X4), scales=scales[1][:], in_=grouped[1][:].rearrange("p c t -> p (c t)"))
-        acc1 = psum.tile([P, 512], F32, name="acc1")
-        nc.tensor.matmul_mx(out=acc1[:, 0:256], lhsT=codes[1][:].bitcast(FP8X4), lhsT_scale=scales[1][:], rhs=picked_words[:, 0:256].bitcast(FP8X4), rhs_scale=picked_bytes0[:], start=True, stop=True)
-        nc.tensor.matmul_mx(out=acc1[:, 256:512], lhsT=codes[1][:].bitcast(FP8X4), lhsT_scale=scales[1][:], rhs=picked_words[:, 256:512].bitcast(FP8X4), rhs_scale=picked_bytes1[:], start=True, stop=True)
-        nc.scalar.copy(grouped[2][:].rearrange("p (c i) t -> p c t i", i=4), h1[:, :, 128:256].rearrange("p t (c i) -> p c t i", i=4))
-        nc.vector.quantize_mx(out=codes[2][:].bitcast(FP8X4), scales=scales[2][:], in_=grouped[2][:].rearrange("p c t -> p (c t)"))
-        acc2 = psum.tile([P, 512], F32, name="acc2")
-        nc.tensor.matmul_mx(out=acc2[:, 0:256], lhsT=codes[2][:].bitcast(FP8X4), lhsT_scale=scales[2][:], rhs=picked_words[:, 0:256].bitcast(FP8X4), rhs_scale=picked_bytes0[:], start=True, stop=True)
-        nc.tensor.matmul_mx(out=acc2[:, 256:512], lhsT=codes[2][:].bitcast(FP8X4), lhsT_scale=scales[2][:], rhs=picked_words[:, 256:512].bitcast(FP8X4), rhs_scale=picked_bytes1[:], start=True, stop=True)
+        acc1_0 = psum.tile([P, 256], F32, name="acc1_0")
+        nc.tensor.matmul_mx(out=acc1_0[:, 0:256], lhsT=codes[1][:].bitcast(FP8X4), lhsT_scale=scales[1][:], rhs=picked_words[:, 0:256].bitcast(FP8X4), rhs_scale=picked_bytes0[:], start=True, stop=True)
+        acc1_1 = psum.tile([P, 256], F32, name="acc1_1")
+        nc.tensor.matmul_mx(out=acc1_1[:, 0:256], lhsT=codes[1][:].bitcast(FP8X4), lhsT_scale=scales[1][:], rhs=picked_words[:, 256:512].bitcast(FP8X4), rhs_scale=picked_bytes1[:], start=True, stop=True)
         nc.scalar.copy(grouped[3][:].rearrange("p (c i) t -> p c t i", i=4), h2[:, :, 0:128].rearrange("p t (c i) -> p c t i", i=4))
+        nc.vector.quantize_mx(out=codes[2][:].bitcast(FP8X4), scales=scales[2][:], in_=grouped[2][:].rearrange("p c t -> p (c t)"))
+        acc2_0 = psum.tile([P, 256], F32, name="acc2_0")
+        nc.tensor.matmul_mx(out=acc2_0[:, 0:256], lhsT=codes[2][:].bitcast(FP8X4), lhsT_scale=scales[2][:], rhs=picked_words[:, 0:256].bitcast(FP8X4), rhs_scale=picked_bytes0[:], start=True, stop=True)
+        acc2_1 = psum.tile([P, 256], F32, name="acc2_1")
+        nc.tensor.matmul_mx(out=acc2_1[:, 0:256], lhsT=codes[2][:].bitcast(FP8X4), lhsT_scale=scales[2][:], rhs=picked_words[:, 256:512].bitcast(FP8X4), rhs_scale=picked_bytes1[:], start=True, stop=True)
         nc.vector.quantize_mx(out=codes[3][:].bitcast(FP8X4), scales=scales[3][:], in_=grouped[3][:].rearrange("p c t -> p (c t)"))
-        acc3 = psum.tile([P, 512], F32, name="acc3")
-        nc.tensor.matmul_mx(out=acc3[:, 0:256], lhsT=codes[3][:].bitcast(FP8X4), lhsT_scale=scales[3][:], rhs=picked_words[:, 0:256].bitcast(FP8X4), rhs_scale=picked_bytes0[:], start=True, stop=True)
-        nc.tensor.matmul_mx(out=acc3[:, 256:512], lhsT=codes[3][:].bitcast(FP8X4), lhsT_scale=scales[3][:], rhs=picked_words[:, 256:512].bitcast(FP8X4), rhs_scale=picked_bytes1[:], start=True, stop=True)
+        acc3_0 = psum.tile([P, 256], F32, name="acc3_0")
+        nc.tensor.matmul_mx(out=acc3_0[:, 0:256], lhsT=codes[3][:].bitcast(FP8X4), lhsT_scale=scales[3][:], rhs=picked_words[:, 0:256].bitcast(FP8X4), rhs_scale=picked_bytes0[:], start=True, stop=True)
+        acc3_1 = psum.tile([P, 256], F32, name="acc3_1")
+        nc.tensor.matmul_mx(out=acc3_1[:, 0:256], lhsT=codes[3][:].bitcast(FP8X4), lhsT_scale=scales[3][:], rhs=picked_words[:, 256:512].bitcast(FP8X4), rhs_scale=picked_bytes1[:], start=True, stop=True)
         z0_0 = keep.tile([P, 256], F32, name="z0_0")
         y0_0 = keep.tile([P, 256], F32, name="y0_0")
         nc.vector.tensor_tensor(z0_0[:], acc0_0[:, 0:256], l0_0[:, 0:256], ALU.subtract)
@@ -101,31 +104,31 @@ def tile_picked_zams_sig_p_kernel(tc, x_words, x_scales, hT, label, offs, out):
         nc.sync.dma_start(out[0:128, 256:512], y0_256[:])
         z1_0 = keep.tile([P, 256], F32, name="z1_0")
         y1_0 = keep.tile([P, 256], F32, name="y1_0")
-        nc.vector.tensor_tensor(z1_0[:], acc1[:, 0:256], l1_0[:, 0:256], ALU.subtract)
+        nc.vector.tensor_tensor(z1_0[:], acc1_0[:, 0:256], l1_0[:, 0:256], ALU.subtract)
         nc.scalar.activation(y1_0[:], z1_0[:], ACT.Sigmoid, scale=4.0)
         nc.sync.dma_start(out[128:256, 0:256], y1_0[:])
         z1_256 = keep.tile([P, 256], F32, name="z1_256")
         y1_256 = keep.tile([P, 256], F32, name="y1_256")
-        nc.vector.tensor_tensor(z1_256[:], acc1[:, 256:512], l1_0[:, 256:512], ALU.subtract)
+        nc.vector.tensor_tensor(z1_256[:], acc1_1[:, 0:256], l1_0[:, 256:512], ALU.subtract)
         nc.scalar.activation(y1_256[:], z1_256[:], ACT.Sigmoid, scale=4.0)
         nc.sync.dma_start(out[128:256, 256:512], y1_256[:])
         z2_0 = keep.tile([P, 256], F32, name="z2_0")
         y2_0 = keep.tile([P, 256], F32, name="y2_0")
-        nc.vector.tensor_tensor(z2_0[:], acc2[:, 0:256], l2_0[:, 0:256], ALU.subtract)
+        nc.vector.tensor_tensor(z2_0[:], acc2_0[:, 0:256], l2_0[:, 0:256], ALU.subtract)
         nc.scalar.activation(y2_0[:], z2_0[:], ACT.Sigmoid, scale=4.0)
         nc.sync.dma_start(out[256:384, 0:256], y2_0[:])
         z2_256 = keep.tile([P, 256], F32, name="z2_256")
         y2_256 = keep.tile([P, 256], F32, name="y2_256")
-        nc.vector.tensor_tensor(z2_256[:], acc2[:, 256:512], l2_0[:, 256:512], ALU.subtract)
+        nc.vector.tensor_tensor(z2_256[:], acc2_1[:, 0:256], l2_0[:, 256:512], ALU.subtract)
         nc.scalar.activation(y2_256[:], z2_256[:], ACT.Sigmoid, scale=4.0)
         nc.sync.dma_start(out[256:384, 256:512], y2_256[:])
         z3_0 = keep.tile([P, 256], F32, name="z3_0")
         y3_0 = keep.tile([P, 256], F32, name="y3_0")
-        nc.vector.tensor_tensor(z3_0[:], acc3[:, 0:256], l3_0[:, 0:256], ALU.subtract)
+        nc.vector.tensor_tensor(z3_0[:], acc3_0[:, 0:256], l3_0[:, 0:256], ALU.subtract)
         nc.scalar.activation(y3_0[:], z3_0[:], ACT.Sigmoid, scale=4.0)
         nc.sync.dma_start(out[384:512, 0:256], y3_0[:])
         z3_256 = keep.tile([P, 256], F32, name="z3_256")
         y3_256 = keep.tile([P, 256], F32, name="y3_256")
-        nc.vector.tensor_tensor(z3_256[:], acc3[:, 256:512], l3_256[:, 0:256], ALU.subtract)
+        nc.vector.tensor_tensor(z3_256[:], acc3_1[:, 0:256], l3_256[:, 0:256], ALU.subtract)
         nc.scalar.activation(y3_256[:], z3_256[:], ACT.Sigmoid, scale=4.0)
         nc.sync.dma_start(out[384:512, 256:512], y3_256[:])

@@ -42,7 +42,7 @@ def tile_picked_zams_sig_p_kernel(tc, x_words, x_scales, hT, label, offs, out):
         nc.sync.dma_start(table_words[:].bitcast(I32), x_words[0].rearrange("p n t -> p (n t)").bitcast(I32))
         nc.sync.dma_start(offsets[:], offs)
         for q in range(4):
-            nc.sync.dma_start(table_bytes[32 * q : 32 * q + 4, :].bitcast(I32), x_scales[0, 4 * q : 4 * q + 4, :].bitcast(I32))
+            nc.sync.dma_start(table_bytes[q:P:32, :].bitcast(I32), x_scales[0, q:16:4, :].bitcast(I32))
         h0 = keep.tile([P, PACK, 128], F32, name="h0", tag="h0", align_bytes=64)
         nc.sync.dma_start(h0[:], h_rows[:, :, 0:128])
         h1 = keep.tile([P, PACK, 256], F32, name="h1", tag="h1", align_bytes=64)

@@ -19,8 +19,11 @@ P = 128
 PACK = 4
 M_TILES = J // P
 HALF = S // 2
-H_LOADS = 2
-H_WIDTH = J // H_LOADS
+H_LOADS = ((0, 1), (1, 2), (3, 1))
+LABEL_LOADS = ((0, 0, 512), (1, 0, 512), (2, 0, 512), (3, 0, 256), (3, 256, 512))
+STORES = ((0, 0, 256), (0, 256, 512), (1, 0, 256), (1, 256, 512), (2, 0, 256), (2, 256, 512), (3, 0, 256), (3, 256, 384), (3, 384, 512))
+PASSES = tuple((m, c, c + 256) for m in range(4) for c in (0, 256))
+PIECES = ((0, 0, 256), (0, 256, 512), (1, 0, 256), (1, 256, 512), (2, 0, 256), (2, 256, 512), (3, 0, 256), (3, 256, 384), (3, 384, 512))
 
 
 def tile_picked_zams_sig_p_kernel(tc, x_words, x_scales, hT, label, offs, out):
@@ -32,103 +35,121 @@ def tile_picked_zams_sig_p_kernel(tc, x_words, x_scales, hT, label, offs, out):
         offsets = keep.tile([P, S // 16], U16, name="offsets")
         table_words = keep.tile([P, T], U32, name="table_words", align_bytes=64)
         table_bytes = keep.tile([P, T], U8, name="table_bytes", align_bytes=64)
-        picked_words = keep.tile([P, S], U32, name="picked_words", align_bytes=64)
         warm_in = keep.tile([P, 1], F32, name="warm_in")
         warm_out = keep.tile([P, 1], F32, name="warm_out")
 
         nc.vector.memset(table_bytes[:].bitcast(I32), 0)
         nc.vector.memset(warm_in[:], 0.0)
         h_rows = hT.rearrange("(p t) c -> p t c", t=PACK)
-        nc.sync.dma_start(table_words[:].bitcast(I32), x_words[0].rearrange("p n t -> p (n t)").bitcast(I32))
-        nc.sync.dma_start(offsets[:], offs)
-        for q in range(4):
-            nc.sync.dma_start(table_bytes[q:P:32, :].bitcast(I32), x_scales[0, q:16:4, :].bitcast(I32))
-        h0 = keep.tile([P, PACK, 128], F32, name="h0", tag="h0", align_bytes=64)
-        nc.sync.dma_start(h0[:], h_rows[:, :, 0:128])
-        h1 = keep.tile([P, PACK, 256], F32, name="h1", tag="h1", align_bytes=64)
-        nc.sync.dma_start(h1[:], h_rows[:, :, 128:384])
-        h2 = keep.tile([P, PACK, 128], F32, name="h2", tag="h2", align_bytes=64)
-        nc.sync.dma_start(h2[:], h_rows[:, :, 384:512])
-        l0_0 = keep.tile([P, 512], F32, name="l0_0")
-        nc.sync.dma_start(l0_0[:], label[0:128, 0:512])
-        l1_0 = keep.tile([P, 512], F32, name="l1_0")
-        nc.sync.dma_start(l1_0[:], label[128:256, 0:512])
-        l2_0 = keep.tile([P, 512], F32, name="l2_0")
-        nc.sync.dma_start(l2_0[:], label[256:384, 0:512])
-        l3_0 = keep.tile([P, 256], F32, name="l3_0")
-        nc.sync.dma_start(l3_0[:], label[384:512, 0:256])
-        l3_256 = keep.tile([P, 256], F32, name="l3_256")
-        nc.sync.dma_start(l3_256[:], label[384:512, 256:512])
+        raw, margins, words, planes, acc = {}, [], [], [], []
+
+        def part(parts, a, b):
+            tile, c0 = [(t, lo) for t, lo, hi in parts if lo <= a and b <= hi][0]
+            return tile[:, a - c0 : b - c0]
+
+        def load_words():
+            nc.sync.dma_start(table_words[:].bitcast(I32), x_words[0].rearrange("p n t -> p (n t)").bitcast(I32))
+
+        def load_list():
+            nc.sync.dma_start(offsets[:], offs)
+
+        def load_scales(queue, rows):
+            for r in rows:
+                queue.dma_start(table_bytes[r:P:32, :].bitcast(I32), x_scales[0, r:16:4, :].bitcast(I32))
+
+        def load_faces(i):
+            first, count = H_LOADS[i]
+            h = keep.tile([P, PACK, count * P], F32, name=f"h{i}", tag=f"h{i}", align_bytes=64)
+            nc.sync.dma_start(h[:], h_rows[:, :, P * first : P * (first + count)])
+            for j in range(count):
+                raw[first + j] = h[:, :, P * j : P * (j + 1)]
+
+        def load_margin(i):
+            m, c0, c1 = LABEL_LOADS[i]
+            lab = keep.tile([P, c1 - c0], F32, name=f"label{i}")
+            nc.sync.dma_start(lab[:], label[P * m : P * (m + 1), c0:c1])
+            margins.append((lab, S * m + c0, S * m + c1))
+
+        load_words()
+        load_list()
+        load_scales(nc.sync, range(4))
+        for i in range(len(H_LOADS)):
+            load_faces(i)
+        for i in range(len(LABEL_LOADS)):
+            load_margin(i)
         nc.scalar.activation(warm_out[:], warm_in[:], ACT.Sigmoid, scale=4.0)
-        grouped = [keep.tile([P, P, PACK], BF16, name=f"grouped{m}", tag=f"grouped{m}", align_bytes=64) for m in range(4)]
-        codes = [keep.tile([P, P], U32, name=f"codes{m}", align_bytes=64) for m in range(4)]
-        scales = [keep.tile([P, P], U8, name=f"scales{m}", align_bytes=64) for m in range(4)]
-        nc.scalar.copy(grouped[0][:].rearrange("p (c i) t -> p c t i", i=4), h0[:, :, 0:128].rearrange("p t (c i) -> p c t i", i=4))
-        nc.vector.tensor_copy(picked_words[:], table_words[:].indirect(offsets[:]))
-        picked_bytes0 = keep.tile([P, 256], U8, name="picked_bytes0", tag="picked_bytes0", align_bytes=64)
-        nc.vector.tensor_copy(picked_bytes0[:], table_bytes[:].indirect(offsets[:, 0:16]))
-        nc.vector.quantize_mx(out=codes[0][:].bitcast(FP8X4), scales=scales[0][:], in_=grouped[0][:].rearrange("p c t -> p (c t)"))
-        picked_bytes1 = keep.tile([P, 256], U8, name="picked_bytes1", tag="h0", align_bytes=64)
-        nc.vector.tensor_copy(picked_bytes1[:], table_bytes[:].indirect(offsets[:, 16:32]))
-        acc0_0 = psum.tile([P, 256], F32, name="acc0_0")
-        nc.tensor.matmul_mx(out=acc0_0[:, 0:256], lhsT=codes[0][:].bitcast(FP8X4), lhsT_scale=scales[0][:], rhs=picked_words[:, 0:256].bitcast(FP8X4), rhs_scale=picked_bytes0[:], start=True, stop=True)
-        acc0_1 = psum.tile([P, 256], F32, name="acc0_1")
-        nc.tensor.matmul_mx(out=acc0_1[:, 0:256], lhsT=codes[0][:].bitcast(FP8X4), lhsT_scale=scales[0][:], rhs=picked_words[:, 256:512].bitcast(FP8X4), rhs_scale=picked_bytes1[:], start=True, stop=True)
-        nc.scalar.copy(grouped[1][:].rearrange("p (c i) t -> p c t i", i=4), h1[:, :, 0:128].rearrange("p t (c i) -> p c t i", i=4))
-        nc.gpsimd.tensor_scalar(grouped[2][:], h1[:, :, 128:256].rearrange("p t c -> p c t"), 1.0, 0.0, ALU.mult, ALU.add)
-        nc.vector.quantize_mx(out=codes[1][:].bitcast(FP8X4), scales=scales[1][:], in_=grouped[1][:].rearrange("p c t -> p (c t)"))
-        acc1_0 = psum.tile([P, 256], F32, name="acc1_0")
-        nc.tensor.matmul_mx(out=acc1_0[:, 0:256], lhsT=codes[1][:].bitcast(FP8X4), lhsT_scale=scales[1][:], rhs=picked_words[:, 0:256].bitcast(FP8X4), rhs_scale=picked_bytes0[:], start=True, stop=True)
-        acc1_1 = psum.tile([P, 256], F32, name="acc1_1")
-        nc.tensor.matmul_mx(out=acc1_1[:, 0:256], lhsT=codes[1][:].bitcast(FP8X4), lhsT_scale=scales[1][:], rhs=picked_words[:, 256:512].bitcast(FP8X4), rhs_scale=picked_bytes1[:], start=True, stop=True)
-        nc.scalar.copy(grouped[3][:].rearrange("p (c i) t -> p c t i", i=4), h2[:, :, 0:128].rearrange("p t (c i) -> p c t i", i=4))
-        nc.vector.quantize_mx(out=codes[2][:].bitcast(FP8X4), scales=scales[2][:], in_=grouped[2][:].rearrange("p c t -> p (c t)"))
-        acc2_0 = psum.tile([P, 256], F32, name="acc2_0")
-        nc.tensor.matmul_mx(out=acc2_0[:, 0:256], lhsT=codes[2][:].bitcast(FP8X4), lhsT_scale=scales[2][:], rhs=picked_words[:, 0:256].bitcast(FP8X4), rhs_scale=picked_bytes0[:], start=True, stop=True)
-        acc2_1 = psum.tile([P, 256], F32, name="acc2_1")
-        nc.tensor.matmul_mx(out=acc2_1[:, 0:256], lhsT=codes[2][:].bitcast(FP8X4), lhsT_scale=scales[2][:], rhs=picked_words[:, 256:512].bitcast(FP8X4), rhs_scale=picked_bytes1[:], start=True, stop=True)
-        nc.vector.quantize_mx(out=codes[3][:].bitcast(FP8X4), scales=scales[3][:], in_=grouped[3][:].rearrange("p c t -> p (c t)"))
-        acc3_0 = psum.tile([P, 256], F32, name="acc3_0")
-        nc.tensor.matmul_mx(out=acc3_0[:, 0:256], lhsT=codes[3][:].bitcast(FP8X4), lhsT_scale=scales[3][:], rhs=picked_words[:, 0:256].bitcast(FP8X4), rhs_scale=picked_bytes0[:], start=True, stop=True)
-        acc3_1 = psum.tile([P, 256], F32, name="acc3_1")
-        nc.tensor.matmul_mx(out=acc3_1[:, 0:256], lhsT=codes[3][:].bitcast(FP8X4), lhsT_scale=scales[3][:], rhs=picked_words[:, 256:512].bitcast(FP8X4), rhs_scale=picked_bytes1[:], start=True, stop=True)
-        z0_0 = keep.tile([P, 256], F32, name="z0_0")
-        y0_0 = keep.tile([P, 256], F32, name="y0_0")
-        nc.vector.tensor_tensor(z0_0[:], acc0_0[:, 0:256], l0_0[:, 0:256], ALU.subtract)
-        nc.scalar.activation(y0_0[:], z0_0[:], ACT.Sigmoid, scale=4.0)
-        nc.sync.dma_start(out[0:128, 0:256], y0_0[:])
-        z0_256 = keep.tile([P, 256], F32, name="z0_256")
-        y0_256 = keep.tile([P, 256], F32, name="y0_256")
-        nc.vector.tensor_tensor(z0_256[:], acc0_1[:, 0:256], l0_0[:, 256:512], ALU.subtract)
-        nc.scalar.activation(y0_256[:], z0_256[:], ACT.Sigmoid, scale=4.0)
-        nc.sync.dma_start(out[0:128, 256:512], y0_256[:])
-        z1_0 = keep.tile([P, 256], F32, name="z1_0")
-        y1_0 = keep.tile([P, 256], F32, name="y1_0")
-        nc.vector.tensor_tensor(z1_0[:], acc1_0[:, 0:256], l1_0[:, 0:256], ALU.subtract)
-        nc.scalar.activation(y1_0[:], z1_0[:], ACT.Sigmoid, scale=4.0)
-        nc.sync.dma_start(out[128:256, 0:256], y1_0[:])
-        z1_256 = keep.tile([P, 256], F32, name="z1_256")
-        y1_256 = keep.tile([P, 256], F32, name="y1_256")
-        nc.vector.tensor_tensor(z1_256[:], acc1_1[:, 0:256], l1_0[:, 256:512], ALU.subtract)
-        nc.scalar.activation(y1_256[:], z1_256[:], ACT.Sigmoid, scale=4.0)
-        nc.sync.dma_start(out[128:256, 256:512], y1_256[:])
-        z2_0 = keep.tile([P, 256], F32, name="z2_0")
-        y2_0 = keep.tile([P, 256], F32, name="y2_0")
-        nc.vector.tensor_tensor(z2_0[:], acc2_0[:, 0:256], l2_0[:, 0:256], ALU.subtract)
-        nc.scalar.activation(y2_0[:], z2_0[:], ACT.Sigmoid, scale=4.0)
-        nc.sync.dma_start(out[256:384, 0:256], y2_0[:])
-        z2_256 = keep.tile([P, 256], F32, name="z2_256")
-        y2_256 = keep.tile([P, 256], F32, name="y2_256")
-        nc.vector.tensor_tensor(z2_256[:], acc2_1[:, 0:256], l2_0[:, 256:512], ALU.subtract)
-        nc.scalar.activation(y2_256[:], z2_256[:], ACT.Sigmoid, scale=4.0)
-        nc.sync.dma_start(out[256:384, 256:512], y2_256[:])
-        z3_0 = keep.tile([P, 256], F32, name="z3_0")
-        y3_0 = keep.tile([P, 256], F32, name="y3_0")
-        nc.vector.tensor_tensor(z3_0[:], acc3_0[:, 0:256], l3_0[:, 0:256], ALU.subtract)
-        nc.scalar.activation(y3_0[:], z3_0[:], ACT.Sigmoid, scale=4.0)
-        nc.sync.dma_start(out[384:512, 0:256], y3_0[:])
-        z3_256 = keep.tile([P, 256], F32, name="z3_256")
-        y3_256 = keep.tile([P, 256], F32, name="y3_256")
-        nc.vector.tensor_tensor(z3_256[:], acc3_1[:, 0:256], l3_256[:, 0:256], ALU.subtract)
-        nc.scalar.activation(y3_256[:], z3_256[:], ACT.Sigmoid, scale=4.0)
-        nc.sync.dma_start(out[384:512, 256:512], y3_256[:])
+
+        grouped = [keep.tile([P, P, PACK], BF16, name=f"grouped{m}", tag=f"grouped{m}", align_bytes=64) for m in range(M_TILES)]
+        codes = [keep.tile([P, P], U32, name=f"codes{m}", align_bytes=64) for m in range(M_TILES)]
+        scales = [keep.tile([P, P], U8, name=f"scales{m}", align_bytes=64) for m in range(M_TILES)]
+        y = [keep.tile([P, S], F32, name=f"y{m}") for m in range(M_TILES)]
+
+        def picked(parts, dtype, a, b, tag):
+            parts.append((keep.tile([P, b - a], dtype, name=f"picked_{tag}_{a}", tag=tag, align_bytes=64), a, b))
+
+        def gather_words(a, b):
+            nc.vector.tensor_copy(part(words, a, b), table_words[:].indirect(offsets[:, a // 16 : b // 16]))
+
+        def gather_bytes(a, b):
+            nc.vector.tensor_copy(part(planes, a, b), table_bytes[:].indirect(offsets[:, a // 16 : b // 16]))
+
+        def interleave_scalar(m, a=0, b=P):
+            nc.scalar.copy(grouped[m][:, a:b, :].rearrange("p (c i) t -> p c t i", i=4), raw[m][:, :, a:b].rearrange("p t (c i) -> p c t i", i=4))
+
+        def interleave_gpsimd(m, a=0, b=P):
+            nc.gpsimd.tensor_scalar(grouped[m][:, a:b, :], raw[m][:, :, a:b].rearrange("p t c -> p c t"), 1.0, 0.0, ALU.mult, ALU.add)
+
+        def quantise(m):
+            nc.vector.quantize_mx(out=codes[m][:].bitcast(FP8X4), scales=scales[m][:], in_=grouped[m][:].rearrange("p c t -> p (c t)"))
+
+        def product(m, a, b, step=None):
+            bank = psum.tile([P, b - a], F32, name=f"acc{m}_{a}")
+            acc.append((bank, S * m + a, S * m + b))
+            step = step or b - a
+            for c in range(a, b, step):
+                nc.tensor.matmul_mx(out=bank[:, c - a : c - a + step], lhsT=codes[m][:].bitcast(FP8X4), lhsT_scale=scales[m][:], rhs=part(words, c, c + step).bitcast(FP8X4), rhs_scale=part(planes, c, c + step), start=True, stop=True)
+
+        def products(m):
+            for mm, a, b in PASSES:
+                if mm == m:
+                    product(m, a, b)
+
+        def squash(m, a, b, z):
+            nc.scalar.activation(y[m][:, a:b], z[:], ACT.Sigmoid, scale=4.0)
+            for mm, c0, c1 in STORES:
+                if mm == m and c1 == b:
+                    nc.sync.dma_start(out[P * m : P * (m + 1), c0:c1], y[m][:, c0:c1])
+
+        def finish(m, a, b):
+            z = keep.tile([P, b - a], F32, name=f"z{m}_{a}")
+            nc.vector.tensor_tensor(z[:], part(acc, S * m + a, S * m + b), part(margins, S * m + a, S * m + b), ALU.subtract)
+            squash(m, a, b, z)
+
+        def evacuate(m, a, b):
+            s = keep.tile([P, b - a], F32, name=f"s{m}_{a}")
+            nc.scalar.copy(s[:], part(acc, S * m + a, S * m + b))
+            z = keep.tile([P, b - a], F32, name=f"z{m}_{a}")
+            nc.gpsimd.tensor_tensor(z[:], s[:], part(margins, S * m + a, S * m + b), ALU.subtract)
+            return z
+
+        picked(words, U32, 0, S, "words")
+        picked(planes, U8, 0, HALF, "planes")
+        interleave_scalar(0)
+        gather_words(0, S)
+        gather_bytes(0, HALF)
+        quantise(0)
+        picked(planes, U8, HALF, S, "h0")
+        gather_bytes(HALF, HALF + P)
+        gather_bytes(HALF + P, S)
+        product(0, 0, HALF)
+        product(0, HALF, S, P)
+        interleave_scalar(1)
+        interleave_gpsimd(2)
+        quantise(1)
+        products(1)
+        interleave_scalar(3)
+        for m in (2, 3):
+            quantise(m)
+            products(m)
+        for piece in PIECES:
+            finish(*piece)

@@ -21,9 +21,9 @@ M_TILES = J // P
 HALF = S // 2
 H_LOADS = ((0, 1), (1, 2), (3, 1))
 LABEL_LOADS = ((0, 0, 512), (1, 0, 512), (2, 0, 512), (3, 0, 256), (3, 256, 512))
-STORES = ((0, 0, 256), (0, 256, 512), (1, 0, 256), (1, 256, 512), (2, 0, 256), (2, 256, 512), (3, 0, 256), (3, 256, 384), (3, 384, 512))
-PASSES = tuple((m, c, c + 256) for m in range(4) for c in (0, 256))
-PIECES = ((0, 0, 256), (0, 256, 512), (1, 0, 256), (1, 256, 512), (2, 0, 256), (2, 256, 512), (3, 0, 256), (3, 256, 384), (3, 384, 512))
+STORES = tuple((m, c, c + 256) for m in range(4) for c in (0, 256))
+PASSES = ((0, 0, 256), (0, 256, 384), (0, 384, 512), (1, 0, 256), (1, 256, 512), (2, 0, 256), (2, 256, 512), (3, 0, 256), (3, 256, 512))
+PIECES = ((0, 0, 256), (0, 256, 384), (0, 384, 512), (1, 0, 256), (1, 256, 512), (2, 0, 256), (2, 256, 512), (3, 0, 256), (3, 256, 512))
 
 
 def tile_picked_zams_sig_p_kernel(tc, x_words, x_scales, hT, label, offs, out):
@@ -55,7 +55,7 @@ def tile_picked_zams_sig_p_kernel(tc, x_words, x_scales, hT, label, offs, out):
 
         def load_scales(queue, rows):
             for r in rows:
-                queue.dma_start(table_bytes[r:P:32, :].bitcast(I32), x_scales[0, r:16:4, :].bitcast(I32))
+                queue.dma_start(table_bytes[32 * r : 32 * r + 4, :].bitcast(I32), x_scales[0, 4 * r : 4 * r + 4, :].bitcast(I32))
 
         def load_faces(i):
             first, count = H_LOADS[i]
@@ -102,12 +102,10 @@ def tile_picked_zams_sig_p_kernel(tc, x_words, x_scales, hT, label, offs, out):
         def quantise(m):
             nc.vector.quantize_mx(out=codes[m][:].bitcast(FP8X4), scales=scales[m][:], in_=grouped[m][:].rearrange("p c t -> p (c t)"))
 
-        def product(m, a, b, step=None):
-            bank = psum.tile([P, b - a], F32, name=f"acc{m}_{a}")
+        def product(m, a, b):
+            bank = psum.tile([P, b - a], F32, name=f"acc{m}_{a}", tag=f"bank{len(acc) % 8}")
             acc.append((bank, S * m + a, S * m + b))
-            step = step or b - a
-            for c in range(a, b, step):
-                nc.tensor.matmul_mx(out=bank[:, c - a : c - a + step], lhsT=codes[m][:].bitcast(FP8X4), lhsT_scale=scales[m][:], rhs=part(words, c, c + step).bitcast(FP8X4), rhs_scale=part(planes, c, c + step), start=True, stop=True)
+            nc.tensor.matmul_mx(out=bank[:], lhsT=codes[m][:].bitcast(FP8X4), lhsT_scale=scales[m][:], rhs=part(words, a, b).bitcast(FP8X4), rhs_scale=part(planes, a, b), start=True, stop=True)
 
         def products(m):
             for mm, a, b in PASSES:
@@ -141,15 +139,18 @@ def tile_picked_zams_sig_p_kernel(tc, x_words, x_scales, hT, label, offs, out):
         picked(planes, U8, HALF, S, "h0")
         gather_bytes(HALF, HALF + P)
         gather_bytes(HALF + P, S)
-        product(0, 0, HALF)
-        product(0, HALF, S, P)
+        products(0)
         interleave_scalar(1)
         interleave_gpsimd(2)
         quantise(1)
         products(1)
         interleave_scalar(3)
-        for m in (2, 3):
-            quantise(m)
-            products(m)
-        for piece in PIECES:
+        quantise(2)
+        products(2)
+        for piece in PIECES[:2]:
+            finish(*piece)
+        quantise(3)
+        finish(*PIECES[2])
+        products(3)
+        for piece in PIECES[3:]:
             finish(*piece)

@@ -23,7 +23,7 @@ H_LOADS = ((0, 1), (1, 2), (3, 1))
 LABEL_LOADS = ((0, 0, 512), (1, 0, 512), (2, 0, 512), (3, 0, 256), (3, 256, 512))
 STORES = tuple((m, c, c + 256) for m in range(4) for c in (0, 256))
 PASSES = ((0, 0, 256), (0, 256, 384), (0, 384, 512), (1, 0, 256), (1, 256, 512), (2, 0, 256), (2, 256, 512), (3, 0, 256), (3, 256, 512))
-PIECES = ((0, 0, 256), (0, 256, 384), (0, 384, 512), (1, 0, 256), (1, 256, 512), (2, 0, 256), (2, 256, 512), (3, 0, 256), (3, 256, 512))
+PIECES = ((0, 0, 256), (0, 256, 384), (0, 384, 512), (1, 0, 256), (1, 256, 512), (2, 0, 256), (2, 256, 512), (3, 0, 128), (3, 128, 256), (3, 256, 384), (3, 384, 512))
 
 
 def tile_picked_zams_sig_p_kernel(tc, x_words, x_scales, hT, label, offs, out):

@@ -23,7 +23,7 @@ H_LOADS = ((0, 1), (1, 2), (3, 1))
 LABEL_LOADS = ((0, 0, 512), (1, 0, 512), (2, 0, 512), (3, 0, 256), (3, 256, 512))
 STORES = tuple((m, c, c + 256) for m in range(4) for c in (0, 256))
 PASSES = ((0, 0, 256), (0, 256, 384), (0, 384, 512), (1, 0, 256), (1, 256, 512), (2, 0, 256), (2, 256, 512), (3, 0, 256), (3, 256, 512))
-PIECES = ((0, 0, 256), (0, 256, 384), (0, 384, 512), (1, 0, 256), (1, 256, 512), (2, 0, 256), (2, 256, 512), (3, 0, 128), (3, 128, 256), (3, 256, 384), (3, 384, 512))
+PIECES = tuple((m, c, c + P) for m in range(M_TILES) for c in range(0, S, P))
 
 
 def tile_picked_zams_sig_p_kernel(tc, x_words, x_scales, hT, label, offs, out):
@@ -147,10 +147,10 @@ def tile_picked_zams_sig_p_kernel(tc, x_words, x_scales, hT, label, offs, out):
         interleave_scalar(3)
         quantise(2)
         products(2)
-        for piece in PIECES[:2]:
+        for piece in PIECES[:3]:
             finish(*piece)
         quantise(3)
-        finish(*PIECES[2])
+        finish(*PIECES[3])
         products(3)
-        for piece in PIECES[3:]:
+        for piece in PIECES[4:]:
             finish(*piece)

@@ -20,7 +20,7 @@ PACK = 4
 M_TILES = J // P
 HALF = S // 2
 H_LOADS = ((0, 1), (1, 2), (3, 1))
-LABEL_LOADS = ((0, 0, 512), (1, 0, 512), (2, 0, 512), (3, 0, 256), (3, 256, 512))
+LABEL_LOADS = ((0, 0, 512), (1, 0, 256), (1, 256, 512), (2, 0, 256), (2, 256, 512), (3, 0, 256), (3, 256, 512))
 STORES = tuple((m, c, c + 256) for m in range(4) for c in (0, 256))
 PASSES = ((0, 0, 256), (0, 256, 384), (0, 384, 512), (1, 0, 256), (1, 256, 512), (2, 0, 256), (2, 256, 512), (3, 0, 256), (3, 256, 512))
 PIECES = tuple((m, c, c + P) for m in range(M_TILES) for c in range(0, S, P))

@@ -18,12 +18,7 @@ ALU = mybir.AluOpType
 P = 128
 PACK = 4
 M_TILES = J // P
-HALF = S // 2
-H_LOADS = ((0, 1), (1, 2), (3, 1))
-LABEL_LOADS = ((0, 0, 512), (1, 0, 256), (1, 256, 512), (2, 0, 256), (2, 256, 512), (3, 0, 256), (3, 256, 512))
-STORES = tuple((m, c, c + 256) for m in range(4) for c in (0, 256))
-PASSES = ((0, 0, 256), (0, 256, 384), (0, 384, 512), (1, 0, 256), (1, 256, 512), (2, 0, 256), (2, 256, 512), (3, 0, 256), (3, 256, 512))
-PIECES = tuple((m, c, c + P) for m in range(M_TILES) for c in range(0, S, P))
+BANKS = 8
 
 
 def tile_picked_zams_sig_p_kernel(tc, x_words, x_scales, hT, label, offs, out):
@@ -37,11 +32,17 @@ def tile_picked_zams_sig_p_kernel(tc, x_words, x_scales, hT, label, offs, out):
         table_bytes = keep.tile([P, T], U8, name="table_bytes", align_bytes=64)
         warm_in = keep.tile([P, 1], F32, name="warm_in")
         warm_out = keep.tile([P, 1], F32, name="warm_out")
-
-        nc.vector.memset(table_bytes[:].bitcast(I32), 0)
-        nc.vector.memset(warm_in[:], 0.0)
+        faces = keep.tile([P, PACK * J], F32, name="faces", align_bytes=64)
+        words = keep.tile([P, S], U32, name="words", align_bytes=64)
+        planes = keep.tile([P, S], U8, name="planes", align_bytes=64)
+        grouped = [keep.tile([P, P, PACK], BF16, name=f"grouped{m}", align_bytes=64) for m in range(M_TILES)]
+        codes = [keep.tile([P, P], U32, name=f"codes{m}", align_bytes=64) for m in range(M_TILES)]
+        scales = [keep.tile([P, P], U8, name=f"scales{m}", align_bytes=64) for m in range(M_TILES)]
+        y = [keep.tile([P, S], F32, name=f"y{m}") for m in range(M_TILES)]
+        h_flat = hT.rearrange("(p t) c -> p (t c)", t=PACK)
         h_rows = hT.rearrange("(p t) c -> p t c", t=PACK)
-        raw, margins, words, planes, acc = {}, [], [], [], []
+        raw = faces[:].rearrange("p (t c) -> p t c", t=PACK)
+        margins, acc = [], []
 
         def part(parts, a, b):
             tile, c0 = [(t, lo) for t, lo, hi in parts if lo <= a and b <= hi][0]
@@ -57,100 +58,96 @@ def tile_picked_zams_sig_p_kernel(tc, x_words, x_scales, hT, label, offs, out):
             for r in rows:
                 queue.dma_start(table_bytes[32 * r : 32 * r + 4, :].bitcast(I32), x_scales[0, 4 * r : 4 * r + 4, :].bitcast(I32))
 
-        def load_faces(i):
-            first, count = H_LOADS[i]
-            h = keep.tile([P, PACK, count * P], F32, name=f"h{i}", tag=f"h{i}", align_bytes=64)
-            nc.sync.dma_start(h[:], h_rows[:, :, P * first : P * (first + count)])
-            for j in range(count):
-                raw[first + j] = h[:, :, P * j : P * (j + 1)]
+        def load_faces_run(a, b):
+            nc.sync.dma_start(faces[:, a:b], h_flat[:, a:b])
 
-        def load_margin(i):
-            m, c0, c1 = LABEL_LOADS[i]
-            lab = keep.tile([P, c1 - c0], F32, name=f"label{i}")
+        def load_faces_columns(a, b):
+            nc.sync.dma_start(raw[:, :, a:b], h_rows[:, :, a:b])
+
+        def load_margin(m, c0, c1):
+            lab = keep.tile([P, c1 - c0], F32, name=f"label{m}_{c0}")
             nc.sync.dma_start(lab[:], label[P * m : P * (m + 1), c0:c1])
             margins.append((lab, S * m + c0, S * m + c1))
 
-        load_words()
-        load_list()
-        load_scales(nc.sync, range(4))
-        for i in range(len(H_LOADS)):
-            load_faces(i)
-        for i in range(len(LABEL_LOADS)):
-            load_margin(i)
-        nc.scalar.activation(warm_out[:], warm_in[:], ACT.Sigmoid, scale=4.0)
-
-        grouped = [keep.tile([P, P, PACK], BF16, name=f"grouped{m}", tag=f"grouped{m}", align_bytes=64) for m in range(M_TILES)]
-        codes = [keep.tile([P, P], U32, name=f"codes{m}", align_bytes=64) for m in range(M_TILES)]
-        scales = [keep.tile([P, P], U8, name=f"scales{m}", align_bytes=64) for m in range(M_TILES)]
-        y = [keep.tile([P, S], F32, name=f"y{m}") for m in range(M_TILES)]
-
-        def picked(parts, dtype, a, b, tag):
-            parts.append((keep.tile([P, b - a], dtype, name=f"picked_{tag}_{a}", tag=tag, align_bytes=64), a, b))
-
         def gather_words(a, b):
-            nc.vector.tensor_copy(part(words, a, b), table_words[:].indirect(offsets[:, a // 16 : b // 16]))
+            nc.vector.tensor_copy(words[:, a:b], table_words[:].indirect(offsets[:, a // 16 : b // 16]))
 
         def gather_bytes(a, b):
-            nc.vector.tensor_copy(part(planes, a, b), table_bytes[:].indirect(offsets[:, a // 16 : b // 16]))
+            nc.vector.tensor_copy(planes[:, a:b], table_bytes[:].indirect(offsets[:, a // 16 : b // 16]))
+
+        def views(m, a, b):
+            dst = grouped[m][:, a:b, :].rearrange("p (c i) t -> p c t i", i=4)
+            src = raw[:, :, P * m + a : P * m + b].rearrange("p t (c i) -> p c t i", i=4)
+            return dst, src
 
         def interleave_scalar(m, a=0, b=P):
-            nc.scalar.copy(grouped[m][:, a:b, :].rearrange("p (c i) t -> p c t i", i=4), raw[m][:, :, a:b].rearrange("p t (c i) -> p c t i", i=4))
+            nc.scalar.copy(*views(m, a, b))
+
+        def interleave_vector(m, a=0, b=P):
+            nc.vector.tensor_copy(*views(m, a, b))
 
         def interleave_gpsimd(m, a=0, b=P):
-            nc.gpsimd.tensor_scalar(grouped[m][:, a:b, :], raw[m][:, :, a:b].rearrange("p t c -> p c t"), 1.0, 0.0, ALU.mult, ALU.add)
+            nc.gpsimd.tensor_scalar(grouped[m][:, a:b, :], raw[:, :, P * m + a : P * m + b].rearrange("p t c -> p c t"), 1.0, 0.0, ALU.mult, ALU.add)
 
         def quantise(m):
             nc.vector.quantize_mx(out=codes[m][:].bitcast(FP8X4), scales=scales[m][:], in_=grouped[m][:].rearrange("p c t -> p (c t)"))
 
         def product(m, a, b):
-            bank = psum.tile([P, b - a], F32, name=f"acc{m}_{a}", tag=f"bank{len(acc) % 8}")
+            bank = psum.tile([P, b - a], F32, name=f"acc{m}_{a}", tag=f"bank{len(acc) % BANKS}")
             acc.append((bank, S * m + a, S * m + b))
-            nc.tensor.matmul_mx(out=bank[:], lhsT=codes[m][:].bitcast(FP8X4), lhsT_scale=scales[m][:], rhs=part(words, a, b).bitcast(FP8X4), rhs_scale=part(planes, a, b), start=True, stop=True)
+            nc.tensor.matmul_mx(out=bank[:], lhsT=codes[m][:].bitcast(FP8X4), lhsT_scale=scales[m][:], rhs=words[:, a:b].bitcast(FP8X4), rhs_scale=planes[:, a:b], start=True, stop=True)
 
-        def products(m):
-            for mm, a, b in PASSES:
-                if mm == m:
-                    product(m, a, b)
-
-        def squash(m, a, b, z):
-            nc.scalar.activation(y[m][:, a:b], z[:], ACT.Sigmoid, scale=4.0)
-            for mm, c0, c1 in STORES:
-                if mm == m and c1 == b:
-                    nc.sync.dma_start(out[P * m : P * (m + 1), c0:c1], y[m][:, c0:c1])
+        def products(m, cuts):
+            for a, b in zip(cuts, cuts[1:]):
+                product(m, a, b)
 
         def finish(m, a, b):
             z = keep.tile([P, b - a], F32, name=f"z{m}_{a}")
             nc.vector.tensor_tensor(z[:], part(acc, S * m + a, S * m + b), part(margins, S * m + a, S * m + b), ALU.subtract)
-            squash(m, a, b, z)
+            nc.scalar.activation(y[m][:, a:b], z[:], ACT.Sigmoid, scale=4.0)
 
-        def evacuate(m, a, b):
-            s = keep.tile([P, b - a], F32, name=f"s{m}_{a}")
-            nc.scalar.copy(s[:], part(acc, S * m + a, S * m + b))
-            z = keep.tile([P, b - a], F32, name=f"z{m}_{a}")
-            nc.gpsimd.tensor_tensor(z[:], s[:], part(margins, S * m + a, S * m + b), ALU.subtract)
-            return z
+        def store(m, a, b):
+            nc.sync.dma_start(out[P * m : P * (m + 1), a:b], y[m][:, a:b])
 
-        picked(words, U32, 0, S, "words")
-        picked(planes, U8, 0, HALF, "planes")
-        interleave_scalar(0)
+        def finish_and_store(m, a, b, width):
+            for c in range(a, b, width):
+                finish(m, c, c + width)
+            store(m, a, b)
+
+        nc.vector.memset(table_bytes[:].bitcast(I32), 0)
+        nc.vector.memset(warm_in[:], 0.0)
+        load_words()
+        load_list()
+        load_scales(nc.sync, range(4))
+        load_faces_columns(0, 256)
+        load_faces_columns(256, 512)
+        load_margin(0, 0, 512)
+        load_margin(1, 0, 256)
+        load_margin(1, 256, 512)
+        load_margin(2, 0, 256)
+        load_margin(2, 256, 512)
+        load_margin(3, 0, 256)
+        load_margin(3, 256, 512)
+        nc.scalar.activation(warm_out[:], warm_in[:], ACT.Sigmoid, scale=4.0)
         gather_words(0, S)
-        gather_bytes(0, HALF)
-        quantise(0)
-        picked(planes, U8, HALF, S, "h0")
-        gather_bytes(HALF, HALF + P)
-        gather_bytes(HALF + P, S)
-        products(0)
+        gather_bytes(0, S)
+        interleave_scalar(0)
         interleave_scalar(1)
-        interleave_gpsimd(2)
+        quantise(0)
+        products(0, (0, 256, 512))
         quantise(1)
-        products(1)
+        products(1, (0, 256, 512))
+        interleave_vector(2)
         interleave_scalar(3)
         quantise(2)
-        products(2)
-        for piece in PIECES[:3]:
-            finish(*piece)
+        products(2, (0, 256, 512))
+        finish_and_store(0, 0, 256, 128)
         quantise(3)
-        finish(*PIECES[3])
-        products(3)
-        for piece in PIECES[4:]:
-            finish(*piece)
+        finish_and_store(0, 256, 512, 128)
+        products(3, (0, 256, 512))
+        finish_and_store(1, 0, 256, 128)
+        finish_and_store(1, 256, 512, 128)
+        finish_and_store(2, 0, 256, 128)
+        finish_and_store(2, 256, 512, 128)
+        finish_and_store(3, 0, 256, 128)
+        finish_and_store(3, 256, 512, 128)

@@ -121,11 +121,11 @@ def tile_picked_zams_sig_p_kernel(tc, x_words, x_scales, hT, label, offs, out):
         load_scales(nc.sync, range(4))
         load_faces_columns(0, 256)
         load_faces_columns(256, 512)
-        load_margin(0, 0, 512)
+        load_margin(0, 0, 256)
+        load_margin(0, 256, 512)
         load_margin(1, 0, 256)
         load_margin(1, 256, 512)
-        load_margin(2, 0, 256)
-        load_margin(2, 256, 512)
+        load_margin(2, 0, 512)
         load_margin(3, 0, 256)
         load_margin(3, 256, 512)
         nc.scalar.activation(warm_out[:], warm_in[:], ACT.Sigmoid, scale=4.0)
@@ -134,17 +134,18 @@ def tile_picked_zams_sig_p_kernel(tc, x_words, x_scales, hT, label, offs, out):
         interleave_scalar(0)
         interleave_scalar(1)
         quantise(0)
-        products(0, (0, 256, 512))
+        products(0, (0, 128, 256, 512))
         quantise(1)
         products(1, (0, 256, 512))
-        interleave_vector(2)
+        interleave_vector(2, 0, 68)
+        interleave_scalar(2, 68, P)
         interleave_scalar(3)
         quantise(2)
-        products(2, (0, 256, 512))
+        products(2, (0, 128, 256, 512))
         finish_and_store(0, 0, 256, 128)
-        quantise(3)
         finish_and_store(0, 256, 512, 128)
-        products(3, (0, 256, 512))
+        quantise(3)
+        products(3, (0, 256, 384, 512))
         finish_and_store(1, 0, 256, 128)
         finish_and_store(1, 256, 512, 128)
         finish_and_store(2, 0, 256, 128)

@@ -17,7 +17,6 @@ ALU = mybir.AluOpType
 
 P = 128
 PACK = 4
-M_TILES = J // P
 BANKS = 8
 
 
@@ -27,26 +26,25 @@ def tile_picked_zams_sig_p_kernel(tc, x_words, x_scales, hT, label, offs, out):
         keep = ctx.enter_context(tc.tile_pool(name="keep", bufs=1))
         psum = ctx.enter_context(tc.psum_pool(name="psum", bufs=1))
 
+        def tile(name, shape, dtype, tag=None):
+            return keep.tile(shape, dtype, name=name, tag=tag or name, align_bytes=64)
+
         offsets = keep.tile([P, S // 16], U16, name="offsets")
-        table_words = keep.tile([P, T], U32, name="table_words", align_bytes=64)
-        table_bytes = keep.tile([P, T], U8, name="table_bytes", align_bytes=64)
-        warm_in = keep.tile([P, 1], F32, name="warm_in")
-        warm_out = keep.tile([P, 1], F32, name="warm_out")
-        faces = keep.tile([P, PACK * J], F32, name="faces", align_bytes=64)
-        words = keep.tile([P, S], U32, name="words", align_bytes=64)
-        planes = keep.tile([P, S], U8, name="planes", align_bytes=64)
-        grouped = [keep.tile([P, P, PACK], BF16, name=f"grouped{m}", align_bytes=64) for m in range(M_TILES)]
-        codes = [keep.tile([P, P], U32, name=f"codes{m}", align_bytes=64) for m in range(M_TILES)]
-        scales = [keep.tile([P, P], U8, name=f"scales{m}", align_bytes=64) for m in range(M_TILES)]
-        y = [keep.tile([P, S], F32, name=f"y{m}") for m in range(M_TILES)]
-        h_flat = hT.rearrange("(p t) c -> p (t c)", t=PACK)
+        table_words = tile("table_words", [P, T], U32)
+        table_bytes = tile("table_bytes", [P, T], U8)
+        warm_in = tile("warm_in", [P, 1], F32)
+        warm_out = tile("warm_out", [P, 1], F32)
         h_rows = hT.rearrange("(p t) c -> p t c", t=PACK)
-        raw = faces[:].rearrange("p (t c) -> p t c", t=PACK)
-        margins, acc = [], []
+        faces, words, planes, margins, acc, diffs, ys = [], [], [], [], [], [], []
+        grouped, codes, scales = {}, {}, {}
+
+        def find(parts, a, b):
+            held, c0 = [(t, lo) for t, lo, hi in parts if lo <= a and b <= hi][0]
+            return held, a - c0, b - c0
 
         def part(parts, a, b):
-            tile, c0 = [(t, lo) for t, lo, hi in parts if lo <= a and b <= hi][0]
-            return tile[:, a - c0 : b - c0]
+            held, lo, hi = find(parts, a, b)
+            return held[:, lo:hi]
 
         def load_words():
             nc.sync.dma_start(table_words[:].bitcast(I32), x_words[0].rearrange("p n t -> p (n t)").bitcast(I32))
@@ -54,31 +52,39 @@ def tile_picked_zams_sig_p_kernel(tc, x_words, x_scales, hT, label, offs, out):
         def load_list():
             nc.sync.dma_start(offsets[:], offs)
 
-        def load_scales(queue, rows):
-            for r in rows:
-                queue.dma_start(table_bytes[32 * r : 32 * r + 4, :].bitcast(I32), x_scales[0, 4 * r : 4 * r + 4, :].bitcast(I32))
+        def load_scales_by_quadrant(q):
+            nc.sync.dma_start(table_bytes[32 * q : 32 * q + 4, :].bitcast(I32), x_scales[0, 4 * q : 4 * q + 4, :].bitcast(I32))
 
-        def load_faces_run(a, b):
-            nc.sync.dma_start(faces[:, a:b], h_flat[:, a:b])
+        def load_scales_by_row(r):
+            nc.sync.dma_start(table_bytes[r:P:32, :].bitcast(I32), x_scales[0, r:16:4, :].bitcast(I32))
 
-        def load_faces_columns(a, b):
-            nc.sync.dma_start(raw[:, :, a:b], h_rows[:, :, a:b])
+        def load_faces(a, b):
+            raw = tile(f"faces{a}", [P, PACK, b - a], F32)
+            nc.sync.dma_start(raw[:], h_rows[:, :, a:b])
+            faces.append((raw, a, b))
 
-        def load_margin(m, c0, c1):
-            lab = keep.tile([P, c1 - c0], F32, name=f"label{m}_{c0}")
-            nc.sync.dma_start(lab[:], label[P * m : P * (m + 1), c0:c1])
-            margins.append((lab, S * m + c0, S * m + c1))
+        def load_margin(m, a, b):
+            lab = tile(f"label{m}_{a}", [P, b - a], F32)
+            nc.sync.dma_start(lab[:], label[P * m : P * (m + 1), a:b])
+            margins.append((lab, S * m + a, S * m + b))
 
-        def gather_words(a, b):
-            nc.vector.tensor_copy(words[:, a:b], table_words[:].indirect(offsets[:, a // 16 : b // 16]))
+        def gather_words(a, b, tag=None):
+            picked = tile(f"words{a}", [P, b - a], U32, tag)
+            nc.vector.tensor_copy(picked[:], table_words[:].indirect(offsets[:, a // 16 : b // 16]))
+            words.append((picked, a, b))
 
-        def gather_bytes(a, b):
-            nc.vector.tensor_copy(planes[:, a:b], table_bytes[:].indirect(offsets[:, a // 16 : b // 16]))
+        def gather_bytes(cuts, tag=None):
+            planes.append((tile(f"planes{cuts[0]}", [P, cuts[-1] - cuts[0]], U8, tag), cuts[0], cuts[-1]))
+            for a, b in zip(cuts, cuts[1:]):
+                nc.vector.tensor_copy(part(planes, a, b), table_bytes[:].indirect(offsets[:, a // 16 : b // 16]))
+
+        def group(m, tag=None):
+            grouped[m] = tile(f"grouped{m}", [P, P, PACK], BF16, tag)
 
         def views(m, a, b):
+            raw, lo, hi = find(faces, P * m + a, P * m + b)
             dst = grouped[m][:, a:b, :].rearrange("p (c i) t -> p c t i", i=4)
-            src = raw[:, :, P * m + a : P * m + b].rearrange("p t (c i) -> p c t i", i=4)
-            return dst, src
+            return dst, raw[:, :, lo:hi].rearrange("p t (c i) -> p c t i", i=4)
 
         def interleave_scalar(m, a=0, b=P):
             nc.scalar.copy(*views(m, a, b))
@@ -87,68 +93,73 @@ def tile_picked_zams_sig_p_kernel(tc, x_words, x_scales, hT, label, offs, out):
             nc.vector.tensor_copy(*views(m, a, b))
 
         def interleave_gpsimd(m, a=0, b=P):
-            nc.gpsimd.tensor_scalar(grouped[m][:, a:b, :], raw[:, :, P * m + a : P * m + b].rearrange("p t c -> p c t"), 1.0, 0.0, ALU.mult, ALU.add)
+            raw, lo, hi = find(faces, P * m + a, P * m + b)
+            nc.gpsimd.tensor_scalar(grouped[m][:, a:b, :], raw[:, :, lo:hi].rearrange("p t c -> p c t"), 1.0, 0.0, ALU.mult, ALU.add)
 
-        def quantise(m):
+        def quantise(m, tag=None):
+            codes[m] = tile(f"codes{m}", [P, P], U32, tag)
+            scales[m] = tile(f"scales{m}", [P, P], U8)
             nc.vector.quantize_mx(out=codes[m][:].bitcast(FP8X4), scales=scales[m][:], in_=grouped[m][:].rearrange("p c t -> p (c t)"))
-
-        def product(m, a, b):
-            bank = psum.tile([P, b - a], F32, name=f"acc{m}_{a}", tag=f"bank{len(acc) % BANKS}")
-            acc.append((bank, S * m + a, S * m + b))
-            nc.tensor.matmul_mx(out=bank[:], lhsT=codes[m][:].bitcast(FP8X4), lhsT_scale=scales[m][:], rhs=words[:, a:b].bitcast(FP8X4), rhs_scale=planes[:, a:b], start=True, stop=True)
 
         def products(m, cuts):
             for a, b in zip(cuts, cuts[1:]):
-                product(m, a, b)
+                bank = psum.tile([P, b - a], F32, name=f"acc{m}_{a}", tag=f"bank{len(acc) % BANKS}")
+                acc.append((bank, S * m + a, S * m + b))
+                nc.tensor.matmul_mx(out=bank[:], lhsT=codes[m][:].bitcast(FP8X4), lhsT_scale=scales[m][:], rhs=part(words, a, b).bitcast(FP8X4), rhs_scale=part(planes, a, b), start=True, stop=True)
 
-        def finish(m, a, b):
-            z = keep.tile([P, b - a], F32, name=f"z{m}_{a}")
-            nc.vector.tensor_tensor(z[:], part(acc, S * m + a, S * m + b), part(margins, S * m + a, S * m + b), ALU.subtract)
-            nc.scalar.activation(y[m][:, a:b], z[:], ACT.Sigmoid, scale=4.0)
+        def subtract(m, a, b, width):
+            diffs.append((tile(f"z{m}_{a}", [P, b - a], F32), S * m + a, S * m + b))
+            for c in range(S * m + a, S * m + b, width):
+                nc.vector.tensor_tensor(part(diffs, c, c + width), part(acc, c, c + width), part(margins, c, c + width), ALU.subtract)
+
+        def squash(m, a, b, width):
+            y = tile(f"y{m}_{a}", [P, b - a], F32)
+            ys.append((y, S * m + a, S * m + b))
+            for c in range(S * m + a, S * m + b, width):
+                nc.scalar.activation(part(ys, c, c + width), part(diffs, c, c + width), ACT.Sigmoid, scale=4.0)
 
         def store(m, a, b):
-            nc.sync.dma_start(out[P * m : P * (m + 1), a:b], y[m][:, a:b])
+            nc.sync.dma_start(out[P * m : P * (m + 1), a:b], part(ys, S * m + a, S * m + b))
 
-        def finish_and_store(m, a, b, width):
-            for c in range(a, b, width):
-                finish(m, c, c + width)
+        def finish(m, a, b, sub_width, act_width):
+            subtract(m, a, b, sub_width)
+            squash(m, a, b, act_width)
             store(m, a, b)
 
         nc.vector.memset(table_bytes[:].bitcast(I32), 0)
         nc.vector.memset(warm_in[:], 0.0)
         load_words()
         load_list()
-        load_scales(nc.sync, range(4))
-        load_faces_columns(0, 256)
-        load_faces_columns(256, 512)
-        load_margin(0, 0, 256)
-        load_margin(0, 256, 512)
-        load_margin(1, 0, 256)
-        load_margin(1, 256, 512)
-        load_margin(2, 0, 512)
-        load_margin(3, 0, 256)
-        load_margin(3, 256, 512)
+        for r in range(4):
+            load_scales_by_row(r)
+        load_faces(0, 192)
+        load_faces(192, 384)
+        load_faces(384, 512)
+        load_margin(0, 0, 512)
+        for m in range(1, 4):
+            load_margin(m, 0, 256)
+            load_margin(m, 256, 512)
         nc.scalar.activation(warm_out[:], warm_in[:], ACT.Sigmoid, scale=4.0)
+        for m in range(4):
+            group(m)
         gather_words(0, S)
-        gather_bytes(0, S)
+        gather_bytes((0, 256))
         interleave_scalar(0)
-        interleave_scalar(1)
+        interleave_scalar(1, 0, 64)
+        interleave_scalar(1, 64, P)
+        interleave_scalar(2)
+        nc.scalar.activation(*views(3, 0, P), ACT.Copy)
         quantise(0)
-        products(0, (0, 128, 256, 512))
+        gather_bytes((256, 384, 512), "faces0")
+        products(0, (0, 128, 256, 384, 512))
         quantise(1)
         products(1, (0, 256, 512))
-        interleave_vector(2, 0, 68)
-        interleave_scalar(2, 68, P)
-        interleave_scalar(3)
         quantise(2)
-        products(2, (0, 128, 256, 512))
-        finish_and_store(0, 0, 256, 128)
-        finish_and_store(0, 256, 512, 128)
+        products(2, (0, 256, 512))
+        finish(0, 0, 256, 128, 128)
+        finish(0, 256, 512, 128, 128)
         quantise(3)
         products(3, (0, 256, 384, 512))
-        finish_and_store(1, 0, 256, 128)
-        finish_and_store(1, 256, 512, 128)
-        finish_and_store(2, 0, 256, 128)
-        finish_and_store(2, 256, 512, 128)
-        finish_and_store(3, 0, 256, 128)
-        finish_and_store(3, 256, 512, 128)
+        for m in (1, 2, 3):
+            finish(m, 0, 256, 128, 128)
+            finish(m, 256, 512, 128, 128)

@@ -27,7 +27,7 @@ def tile_picked_zams_sig_p_kernel(tc, x_words, x_scales, hT, label, offs, out):
         psum = ctx.enter_context(tc.psum_pool(name="psum", bufs=1))
 
         def tile(name, shape, dtype, tag=None):
-            return keep.tile(shape, dtype, name=name, tag=tag or name, align_bytes=64)
+            return keep.tile(shape, dtype, name=name, tag=tag or name, align_bytes=256)
 
         offsets = keep.tile([P, S // 16], U16, name="offsets")
         table_words = tile("table_words", [P, T], U32)
@@ -148,7 +148,7 @@ def tile_picked_zams_sig_p_kernel(tc, x_words, x_scales, hT, label, offs, out):
         interleave_scalar(1, 0, 64)
         interleave_scalar(1, 64, P)
         interleave_scalar(2)
-        nc.scalar.activation(*views(3, 0, P), ACT.Copy)
+        interleave_scalar(3)
         quantise(0)
         gather_bytes((256, 384, 512), "faces0")
         products(0, (0, 128, 256, 384, 512))

from contextlib import ExitStack

import concourse.mybir as mybir

K, T, S, J = 512, 1024, 512, 512
FLOPS = 2 * K * S * J

F32 = mybir.dt.float32
BF16 = mybir.dt.bfloat16
I32 = mybir.dt.int32
U32 = mybir.dt.uint32
U16 = mybir.dt.uint16
U8 = mybir.dt.uint8
FP8X4 = mybir.dt.float8_e4m3fn_x4
ACT = mybir.ActivationFunctionType
ALU = mybir.AluOpType

P = 128
PACK = 4
BANKS = 8


def tile_picked_zams_sig_p_kernel(tc, x_words, x_scales, hT, label, offs, out):
    nc = tc.nc
    with ExitStack() as ctx:
        keep = ctx.enter_context(tc.tile_pool(name="keep", bufs=1))
        psum = ctx.enter_context(tc.psum_pool(name="psum", bufs=1))

        def tile(name, shape, dtype, tag=None):
            return keep.tile(shape, dtype, name=name, tag=tag or name, align_bytes=256)

        offsets = keep.tile([P, S // 16], U16, name="offsets")
        table_words = tile("table_words", [P, T], U32)
        table_bytes = tile("table_bytes", [P, T], U8)
        warm_in = tile("warm_in", [P, 1], F32)
        warm_out = tile("warm_out", [P, 1], F32)
        h_rows = hT.rearrange("(p t) c -> p t c", t=PACK)
        faces, words, planes, margins, acc, diffs, ys = [], [], [], [], [], [], []
        grouped, codes, scales = {}, {}, {}

        def find(parts, a, b):
            held, c0 = [(t, lo) for t, lo, hi in parts if lo <= a and b <= hi][0]
            return held, a - c0, b - c0

        def part(parts, a, b):
            held, lo, hi = find(parts, a, b)
            return held[:, lo:hi]

        def load_words():
            nc.sync.dma_start(table_words[:].bitcast(I32), x_words[0].rearrange("p n t -> p (n t)").bitcast(I32))

        def load_list():
            nc.sync.dma_start(offsets[:], offs)

        def load_scales_by_quadrant(q):
            nc.sync.dma_start(table_bytes[32 * q : 32 * q + 4, :].bitcast(I32), x_scales[0, 4 * q : 4 * q + 4, :].bitcast(I32))

        def load_scales_by_row(r):
            nc.sync.dma_start(table_bytes[r:P:32, :].bitcast(I32), x_scales[0, r:16:4, :].bitcast(I32))

        def load_faces(a, b):
            raw = tile(f"faces{a}", [P, PACK, b - a], F32)
            nc.sync.dma_start(raw[:], h_rows[:, :, a:b])
            faces.append((raw, a, b))

        def load_margin(m, a, b):
            lab = tile(f"label{m}_{a}", [P, b - a], F32)
            nc.sync.dma_start(lab[:], label[P * m : P * (m + 1), a:b])
            margins.append((lab, S * m + a, S * m + b))

        def gather_words(a, b, tag=None):
            picked = tile(f"words{a}", [P, b - a], U32, tag)
            nc.vector.tensor_copy(picked[:], table_words[:].indirect(offsets[:, a // 16 : b // 16]))
            words.append((picked, a, b))

        def gather_bytes(cuts, tag=None):
            planes.append((tile(f"planes{cuts[0]}", [P, cuts[-1] - cuts[0]], U8, tag), cuts[0], cuts[-1]))
            for a, b in zip(cuts, cuts[1:]):
                nc.vector.tensor_copy(part(planes, a, b), table_bytes[:].indirect(offsets[:, a // 16 : b // 16]))

        def group(m, tag=None):
            grouped[m] = tile(f"grouped{m}", [P, P, PACK], BF16, tag)

        def views(m, a, b):
            raw, lo, hi = find(faces, P * m + a, P * m + b)
            dst = grouped[m][:, a:b, :].rearrange("p (c i) t -> p c t i", i=4)
            return dst, raw[:, :, lo:hi].rearrange("p t (c i) -> p c t i", i=4)

        def interleave_scalar(m, a=0, b=P):
            nc.scalar.copy(*views(m, a, b))

        def interleave_vector(m, a=0, b=P):
            nc.vector.tensor_copy(*views(m, a, b))

        def interleave_gpsimd(m, a=0, b=P):
            raw, lo, hi = find(faces, P * m + a, P * m + b)
            nc.gpsimd.tensor_scalar(grouped[m][:, a:b, :], raw[:, :, lo:hi].rearrange("p t c -> p c t"), 1.0, 0.0, ALU.mult, ALU.add)

        def quantise(m, tag=None):
            codes[m] = tile(f"codes{m}", [P, P], U32, tag)
            scales[m] = tile(f"scales{m}", [P, P], U8)
            nc.vector.quantize_mx(out=codes[m][:].bitcast(FP8X4), scales=scales[m][:], in_=grouped[m][:].rearrange("p c t -> p (c t)"))

        def products(m, cuts):
            for a, b in zip(cuts, cuts[1:]):
                bank = psum.tile([P, b - a], F32, name=f"acc{m}_{a}", tag=f"bank{len(acc) % BANKS}")
                acc.append((bank, S * m + a, S * m + b))
                nc.tensor.matmul_mx(out=bank[:], lhsT=codes[m][:].bitcast(FP8X4), lhsT_scale=scales[m][:], rhs=part(words, a, b).bitcast(FP8X4), rhs_scale=part(planes, a, b), start=True, stop=True)

        def subtract(m, a, b, width):
            diffs.append((tile(f"z{m}_{a}", [P, b - a], F32), S * m + a, S * m + b))
            for c in range(S * m + a, S * m + b, width):
                nc.vector.tensor_tensor(part(diffs, c, c + width), part(acc, c, c + width), part(margins, c, c + width), ALU.subtract)

        def squash(m, a, b, width):
            y = tile(f"y{m}_{a}", [P, b - a], F32)
            ys.append((y, S * m + a, S * m + b))
            for c in range(S * m + a, S * m + b, width):
                nc.scalar.activation(part(ys, c, c + width), part(diffs, c, c + width), ACT.Sigmoid, scale=4.0)

        def store(m, a, b):
            nc.sync.dma_start(out[P * m : P * (m + 1), a:b], part(ys, S * m + a, S * m + b))

        def finish(m, a, b, sub_width, act_width):
            subtract(m, a, b, sub_width)
            squash(m, a, b, act_width)
            store(m, a, b)

        nc.vector.memset(table_bytes[:].bitcast(I32), 0)
        nc.vector.memset(warm_in[:], 0.0)
        load_words()
        load_list()
        for r in range(4):
            load_scales_by_row(r)
        load_faces(0, 192)
        load_faces(192, 384)
        load_faces(384, 512)
        load_margin(0, 0, 512)
        for m in range(1, 4):
            load_margin(m, 0, 256)
            load_margin(m, 256, 512)
        nc.scalar.activation(warm_out[:], warm_in[:], ACT.Sigmoid, scale=4.0)
        for m in range(4):
            group(m)
        gather_words(0, S)
        gather_bytes((0, 256))
        interleave_scalar(0)
        interleave_scalar(1, 0, 64)
        interleave_scalar(1, 64, P)
        interleave_scalar(2)
        interleave_scalar(3)
        quantise(0)
        gather_bytes((256, 384, 512), "faces0")
        products(0, (0, 128, 256, 384, 512))
        quantise(1)
        products(1, (0, 256, 512))
        quantise(2)
        products(2, (0, 256, 512))
        finish(0, 0, 256, 128, 128)
        finish(0, 256, 512, 128, 128)
        quantise(3)
        products(3, (0, 256, 384, 512))
        for m in (1, 2, 3):
            finish(m, 0, 256, 128, 128)
            finish(m, 256, 512, 128, 128)
